import numpy as np
CORES = [242,247,114,119]
N = 4
T, CAP = 2048, 64
def entries(a): return a.T.reshape(-1)
def pack(v, P): return np.ascontiguousarray(np.asarray(v, np.int32).reshape(-1, P).T)
def lists(rng, how):
    L = rng.integers(0, T, (N, N, CAP))
    if how == "alike": L[:] = rng.integers(0, T, (N, N, 1))
    if how == "distinct": L = np.stack([np.stack([rng.permutation(T)[:CAP] for d in range(N)]) for r in range(N)])
    if how == "sorted": L = np.sort(L, axis=2)
    if how == "edge": L = np.where(rng.random((N, N, CAP)) < 0.5, 0, T - 1)
    return {"l": np.stack([pack(L[r].reshape(-1), 16) for r in range(N)])}
def setup_inputs(rng):
    return dict({"x": rng.standard_normal((N, 128, T), dtype=np.float32)}, **lists(rng, "uniform"))
def setup_inputs_alike(rng):
    d = setup_inputs(rng); d.update(lists(rng, "alike"))
    for k in ("x",): d[k] = (d[k].astype(np.float32) * 1048576.0).astype(d[k].dtype)
    return d
def setup_inputs_distinct(rng):
    d = setup_inputs(rng); d.update(lists(rng, "distinct"))
    for k in ("x",): d[k] = (d[k].astype(np.float32) * (1 / 1024.0)).astype(d[k].dtype)
    return d
def setup_inputs_edge(rng):
    d = setup_inputs(rng); d.update(lists(rng, "edge"))
    return d
def setup_inputs_sorted(rng):
    d = setup_inputs(rng); d.update(lists(rng, "sorted"))
    return d
def check_inputs(x):
    bad = []
    if x["l"].min() < 0 or x["l"].max() >= T: bad.append("l out of range")
    return bad
def reference(x, l):
    y = np.zeros((N, 128, N * CAP), x.dtype)
    for r in range(N):
        L = entries(l[r])
        for d in range(N): y[d][:, CAP * r:CAP * r + CAP] = x[r][:, L[CAP * d:CAP * d + CAP]]
    return {"y": y}

@@ -1,0 +1,118 @@
+from concourse.bass import DstId, RemoteDMATransfer
+from concourse.mybir import AluOpType
+
+P = 128
+COLS = 2048
+CAP = 64
+LP = 16
+LC = CAP // LP
+
+SCRATCH = {
+    "xs": ("sbuf", [P, COLS], "float32"),
+    "li": ("sbuf", [P, 4 * LC], "int32"),
+    "lf": ("sbuf", [P, 4 * LC], "float32"),
+    "rep": ("sbuf", [P, P], "float32"),
+    "ps": ("psum", [P, 4 * LC], "float32"),
+    "off": ("sbuf", [P, 4 * LC], "uint16"),
+    "gat": ("sbuf", [P, 4 * CAP], "float32"),
+    "land": ("sbuf", [P, 4 * CAP], "float32"),
+}
+SEMAPHORES = ["l_in", "x_in", "ones", "rep_ok", "lf_ok", "mm_ok", "off_ok", "g_far", "g_near", "g_own",
+              "sent", "a_far", "a_near", "st_far", "st_home"]
+
+
+def _bits(mask):
+    return [e for e in range(mask.bit_length()) if (mask >> e) & 1]
+
+
+def _mask(engines):
+    return sum(1 << e for e in engines)
+
+
+def _runs(ranks):
+    out = []
+    for r in sorted(ranks):
+        if out and out[-1][1] == r:
+            out[-1] = (out[-1][0], r + 1)
+        else:
+            out.append((r, r + 1))
+    return out
+
+
+def _plan(rank, cores, topo):
+    me = cores[rank]
+    home = lambda c: (topo.host(c), topo.chip(c)) == (topo.host(me), topo.chip(me))
+    far = [d for d in range(len(cores)) if d != rank and not home(cores[d])]
+    near = [d for d in range(len(cores)) if d != rank and home(cores[d])]
+    out_eng = _bits(min(topo.mask(me, cores[d]) for d in far))
+    k = len(out_eng) // len(far)
+    far_plan = [(d, _mask(out_eng[i * k:(i + 1) * k])) for i, d in enumerate(far)]
+    rest = [e for e in _bits(min(topo.mask(me, cores[d]) for d in near)) if e not in out_eng]
+    k = len(rest) // len(near)
+    near_plan = [(d, _mask(rest[i * k:(i + 1) * k])) for i, d in enumerate(near)]
+    return far_plan, near_plan
+
+
+def rank_program(g, core, T, topo):
+    rank = T.rank_of(core)
+    if rank is None:
+        return
+    S, v, cores = T.sem, g.vector, T.cores
+    far, near = _plan(rank, cores, topo)
+    blk = lambda t, lo, hi: t[:, CAP * lo:CAP * hi]
+    pick = lambda lo, hi: T.xs[:, 0:COLS].indirect(T.off[:, LC * lo:LC * hi])
+
+    g.sync.dma_start(T.li[0:LP, :], T.l[:, :]).then_inc(S.l_in, 16)
+    g.scalar.dma_start(T.xs[0:P // 2, :], T.x[0:P // 2, :]).then_inc(S.x_in, 16)
+    g.sync.dma_start(T.xs[P // 2:P, :], T.x[P // 2:P, :]).then_inc(S.x_in, 16)
+
+    v.memset(T.rep[0:LP, :], 1.0).then_inc(S.ones, 1)
+    g.wait_ge(S.ones, 1)
+    g.affine_select(T.rep[0:LP, :], T.rep[0:LP, :], [[0, P // LP], [-1, LP]], AluOpType.is_equal, 0.0, 0, 1).then_inc(S.rep_ok, 1)
+    v.wait_ge(S.l_in, 16)
+    v.tensor_copy(T.lf[0:LP, :], T.li[0:LP, :]).then_inc(S.lf_ok, 1)
+    g.tensor.wait_ge(S.rep_ok, 1)
+    g.tensor.wait_ge(S.lf_ok, 1)
+    g.tensor.matmul(T.ps[:, :], T.rep[0:LP, :], T.lf[0:LP, :], True, True).then_inc(S.mm_ok, 1)
+    v.wait_ge(S.mm_ok, 1)
+    v.tensor_copy(T.off[:, :], T.ps[:, :]).then_inc(S.off_ok, 1)
+    v.wait_ge(S.off_ok, 1)
+    v.wait_ge(S.x_in, 32)
+
+    far_runs = _runs([d for d, _ in far])
+    for lo, hi in far_runs:
+        v.tensor_copy(blk(T.gat, lo, hi), pick(lo, hi)).then_inc(S.g_far, 1)
+    near_runs = _runs([d for d, _ in near])
+    for lo, hi in near_runs:
+        v.tensor_copy(blk(T.gat, lo, hi), pick(lo, hi)).then_inc(S.g_near, 1)
+    v.tensor_copy(blk(T.land, rank, rank + 1), pick(rank, rank + 1)).then_inc(S.g_own, 1)
+
+    def transfer(d, m, sem):
+        rid, pid = topo.addr(cores[d], core)
+        return RemoteDMATransfer(dst_ids=[DstId(rid=rid, pnc=pid)], dma_engine_mask=m, remote_sem=sem,
+                                 src=blk(T.gat, d, d + 1), dst=blk(T.land, rank, rank + 1))
+    g.wait_ge(S.g_far, len(far_runs))
+    g.remote_dma_fused([transfer(d, m, S.a_far) for d, m in far], local_sem=S.sent)
+    g.wait_ge(S.g_near, len(near_runs))
+    g.remote_dma_fused([transfer(d, m, S.a_near) for d, m in near], local_sem=S.sent)
+
+    def arrives(senders, which):
+        return sum(len(_bits(m)) for s in senders for d, m in _plan(s, cores, topo)[which] if d == rank)
+    far_src = [d for d, _ in far]
+    g.sync.wait_ge(S.a_far, arrives(far_src, 0))
+    n = 0
+    for lo, hi in _runs(far_src):
+        g.sync.dma_start(blk(T.y, lo, hi), blk(T.land, lo, hi)).then_inc(S.st_far, 16)
+        n += 16
+    g.sync.wait_ge(S.st_far, n)
+
+    near_src = [d for d, _ in near]
+    g.scalar.wait_ge(S.g_own, 1)
+    g.scalar.wait_ge(S.a_near, arrives(near_src, 1))
+    n = 0
+    for lo, hi in _runs(near_src + [rank]):
+        g.scalar.dma_start(blk(T.y, lo, hi), blk(T.land, lo, hi)).then_inc(S.st_home, 16)
+        n += 16
+    g.scalar.wait_ge(S.st_home, n)
+
+    g.wait_ge(S.sent, sum(len(_bits(m)) for _, m in far + near))

@@ -3,22 +3,31 @@ from concourse.mybir import AluOpType
 
 P = 128
 COLS = 2048
+C0 = 512
 CAP = 64
 LP = 16
 LC = CAP // LP
+NL = 4 * LC
+EB = CAP + LC
 
 SCRATCH = {
     "xs": ("sbuf", [P, COLS], "float32"),
-    "li": ("sbuf", [P, 4 * LC], "int32"),
-    "lf": ("sbuf", [P, 4 * LC], "float32"),
+    "li": ("sbuf", [P, NL], "int32"),
+    "lf": ("sbuf", [P, NL + LC], "float32"),
     "rep": ("sbuf", [P, P], "float32"),
-    "ps": ("psum", [P, 4 * LC], "float32"),
-    "off": ("sbuf", [P, 4 * LC], "uint16"),
+    "ps": ("psum", [P, NL + LC], "float32"),
+    "off": ("sbuf", [P, NL], "uint16"),
+    "off0": ("sbuf", [P, LC], "uint16"),
+    "off1": ("sbuf", [P, LC], "uint16"),
+    "tmp": ("sbuf", [P, LC], "float32"),
     "gat": ("sbuf", [P, 4 * CAP], "float32"),
+    "gat0": ("sbuf", [P, EB], "float32"),
+    "pair": ("sbuf", [P, EB + CAP], "float32"),
+    "sel": ("sbuf", [P, LC], "uint16"),
     "land": ("sbuf", [P, 4 * CAP], "float32"),
 }
-SEMAPHORES = ["l_in", "x_in", "ones", "rep_ok", "lf_ok", "mm_ok", "off_ok", "g_far", "g_near", "g_own",
-              "sent", "a_far", "a_near", "st_far", "st_home"]
+SEMAPHORES = ["l_in", "x0_in", "x1_in", "ones", "rep_ok", "lf_ok", "mm_ok", "prep", "g0_ok", "g_far", "g_near", "g_own",
+              "sent", "a_far", "a_n0", "a_n1", "sel_ok", "fin_ok", "st_far", "st_home"]
 
 
 def _bits(mask):
@@ -43,14 +52,12 @@ def _plan(rank, cores, topo):
     me = cores[rank]
     home = lambda c: (topo.host(c), topo.chip(c)) == (topo.host(me), topo.chip(me))
     far = [d for d in range(len(cores)) if d != rank and not home(cores[d])]
-    near = [d for d in range(len(cores)) if d != rank and home(cores[d])]
+    near = [d for d in range(len(cores)) if d != rank and home(cores[d])][0]
     out_eng = _bits(min(topo.mask(me, cores[d]) for d in far))
     k = len(out_eng) // len(far)
     far_plan = [(d, _mask(out_eng[i * k:(i + 1) * k])) for i, d in enumerate(far)]
-    rest = [e for e in _bits(min(topo.mask(me, cores[d]) for d in near)) if e not in out_eng]
-    k = len(rest) // len(near)
-    near_plan = [(d, _mask(rest[i * k:(i + 1) * k])) for i, d in enumerate(near)]
-    return far_plan, near_plan
+    every = topo.mask(me, cores[near])
+    return far_plan, (near, every, _mask([e for e in _bits(every) if e not in out_eng]))
 
 
 def rank_program(g, core, T, topo):
@@ -58,61 +65,77 @@ def rank_program(g, core, T, topo):
     if rank is None:
         return
     S, v, cores = T.sem, g.vector, T.cores
-    far, near = _plan(rank, cores, topo)
+    far, (near, m_early, m_late) = _plan(rank, cores, topo)
     blk = lambda t, lo, hi: t[:, CAP * lo:CAP * hi]
     pick = lambda lo, hi: T.xs[:, 0:COLS].indirect(T.off[:, LC * lo:LC * hi])
+    nl = T.ps[:, LC * near:LC * (near + 1)]
 
+    g.scalar.dma_start(T.xs[:, 0:C0], T.x[:, 0:C0]).then_inc(S.x0_in, 16)
     g.sync.dma_start(T.li[0:LP, :], T.l[:, :]).then_inc(S.l_in, 16)
-    g.scalar.dma_start(T.xs[0:P // 2, :], T.x[0:P // 2, :]).then_inc(S.x_in, 16)
-    g.sync.dma_start(T.xs[P // 2:P, :], T.x[P // 2:P, :]).then_inc(S.x_in, 16)
+    g.scalar.dma_start(T.xs[0:P // 2, C0:COLS], T.x[0:P // 2, C0:COLS]).then_inc(S.x1_in, 16)
+    g.sync.dma_start(T.xs[P // 2:P, C0:COLS], T.x[P // 2:P, C0:COLS]).then_inc(S.x1_in, 16)
 
     v.memset(T.rep[0:LP, :], 1.0).then_inc(S.ones, 1)
+    g.iota(T.lf[0:LP, NL:NL + LC], [[LP, LC]], 0, 1, allow_small_or_imprecise_dtypes=True).then_inc(S.rep_ok, 1)
     g.wait_ge(S.ones, 1)
     g.affine_select(T.rep[0:LP, :], T.rep[0:LP, :], [[0, P // LP], [-1, LP]], AluOpType.is_equal, 0.0, 0, 1).then_inc(S.rep_ok, 1)
     v.wait_ge(S.l_in, 16)
-    v.tensor_copy(T.lf[0:LP, :], T.li[0:LP, :]).then_inc(S.lf_ok, 1)
-    g.tensor.wait_ge(S.rep_ok, 1)
+    v.tensor_copy(T.lf[0:LP, 0:NL], T.li[0:LP, :]).then_inc(S.lf_ok, 1)
+    g.tensor.wait_ge(S.rep_ok, 2)
     g.tensor.wait_ge(S.lf_ok, 1)
     g.tensor.matmul(T.ps[:, :], T.rep[0:LP, :], T.lf[0:LP, :], True, True).then_inc(S.mm_ok, 1)
     v.wait_ge(S.mm_ok, 1)
-    v.tensor_copy(T.off[:, :], T.ps[:, :]).then_inc(S.off_ok, 1)
-    v.wait_ge(S.off_ok, 1)
-    v.wait_ge(S.x_in, 32)
+    v.tensor_scalar(T.off0[:, :], nl, float(C0 - 1), None, AluOpType.min).then_inc(S.prep, 1)
+    v.tensor_scalar(T.tmp[:, :], nl, float(C0), float(EB), AluOpType.is_ge, AluOpType.mult).then_inc(S.prep, 1)
+    v.tensor_copy(T.off[:, :], T.ps[:, 0:NL]).then_inc(S.prep, 1)
+    v.tensor_scalar(T.off1[:, :], nl, float(C0), 0.0, AluOpType.subtract, AluOpType.max).then_inc(S.prep, 1)
+    v.wait_ge(S.prep, 4)
+    v.tensor_tensor(T.gat0[:, CAP:EB], T.tmp[:, :], T.ps[:, NL:NL + LC], AluOpType.add).then_inc(S.g0_ok, 1)
 
+    v.wait_ge(S.x0_in, 16)
+    v.tensor_copy(T.gat0[:, 0:CAP], T.xs[:, 0:C0].indirect(T.off0[:, :])).then_inc(S.g0_ok, 1)
+    rid, pid = topo.addr(cores[near], core)
+    g.wait_ge(S.g0_ok, 2)
+    g.remote_dma(T.pair[:, 0:EB], T.gat0[:, :], S.a_n0, S.sent, pid, rid, m_early)
+
+    v.wait_ge(S.x1_in, 32)
     far_runs = _runs([d for d, _ in far])
     for lo, hi in far_runs:
         v.tensor_copy(blk(T.gat, lo, hi), pick(lo, hi)).then_inc(S.g_far, 1)
-    near_runs = _runs([d for d, _ in near])
-    for lo, hi in near_runs:
-        v.tensor_copy(blk(T.gat, lo, hi), pick(lo, hi)).then_inc(S.g_near, 1)
-    v.tensor_copy(blk(T.land, rank, rank + 1), pick(rank, rank + 1)).then_inc(S.g_own, 1)
 
-    def transfer(d, m, sem):
-        rid, pid = topo.addr(cores[d], core)
-        return RemoteDMATransfer(dst_ids=[DstId(rid=rid, pnc=pid)], dma_engine_mask=m, remote_sem=sem,
+    def transfer(d, m):
+        r, p = topo.addr(cores[d], core)
+        return RemoteDMATransfer(dst_ids=[DstId(rid=r, pnc=p)], dma_engine_mask=m, remote_sem=S.a_far,
                                  src=blk(T.gat, d, d + 1), dst=blk(T.land, rank, rank + 1))
     g.wait_ge(S.g_far, len(far_runs))
-    g.remote_dma_fused([transfer(d, m, S.a_far) for d, m in far], local_sem=S.sent)
-    g.wait_ge(S.g_near, len(near_runs))
-    g.remote_dma_fused([transfer(d, m, S.a_near) for d, m in near], local_sem=S.sent)
+    g.remote_dma_fused([transfer(d, m) for d, m in far], local_sem=S.sent)
 
-    def arrives(senders, which):
-        return sum(len(_bits(m)) for s in senders for d, m in _plan(s, cores, topo)[which] if d == rank)
+    v.tensor_copy(blk(T.gat, near, near + 1), T.xs[:, C0:COLS].indirect(T.off1[:, :])).then_inc(S.g_near, 1)
+    g.wait_ge(S.g_near, 1)
+    g.remote_dma(T.pair[:, EB:EB + CAP], blk(T.gat, near, near + 1), S.a_n1, S.sent, pid, rid, m_late)
+    v.tensor_copy(blk(T.land, rank, rank + 1), pick(rank, rank + 1)).then_inc(S.g_own, 1)
+
+    _, (_, n_early, n_late) = _plan(near, cores, topo)
+    v.wait_ge(S.a_n0, len(_bits(n_early)))
+    v.tensor_copy(T.sel[:, :], T.pair[:, CAP:EB]).then_inc(S.sel_ok, 1)
+    v.wait_ge(S.sel_ok, 1)
+    v.wait_ge(S.a_n1, len(_bits(n_late)))
+    v.tensor_copy(blk(T.land, near, near + 1), T.pair[:, :].indirect(T.sel[:, :])).then_inc(S.fin_ok, 1)
+
     far_src = [d for d, _ in far]
-    g.sync.wait_ge(S.a_far, arrives(far_src, 0))
+    g.sync.wait_ge(S.a_far, sum(len(_bits(m)) for s in far_src for d, m in _plan(s, cores, topo)[0] if d == rank))
     n = 0
     for lo, hi in _runs(far_src):
         g.sync.dma_start(blk(T.y, lo, hi), blk(T.land, lo, hi)).then_inc(S.st_far, 16)
         n += 16
     g.sync.wait_ge(S.st_far, n)
 
-    near_src = [d for d, _ in near]
     g.scalar.wait_ge(S.g_own, 1)
-    g.scalar.wait_ge(S.a_near, arrives(near_src, 1))
+    g.scalar.wait_ge(S.fin_ok, 1)
     n = 0
-    for lo, hi in _runs(near_src + [rank]):
+    for lo, hi in _runs([near, rank]):
         g.scalar.dma_start(blk(T.y, lo, hi), blk(T.land, lo, hi)).then_inc(S.st_home, 16)
         n += 16
     g.scalar.wait_ge(S.st_home, n)
 
-    g.wait_ge(S.sent, sum(len(_bits(m)) for _, m in far + near))
+    g.wait_ge(S.sent, sum(len(_bits(m)) for _, m in far) + len(_bits(m_early)) + len(_bits(m_late)))

from concourse.bass import DstId, RemoteDMATransfer
from concourse.mybir import AluOpType

P = 128
COLS = 2048
C0 = 512
CAP = 64
LP = 16
LC = CAP // LP
NL = 4 * LC
EB = CAP + LC

SCRATCH = {
    "xs": ("sbuf", [P, COLS], "float32"),
    "li": ("sbuf", [P, NL], "int32"),
    "lf": ("sbuf", [P, NL + LC], "float32"),
    "rep": ("sbuf", [P, P], "float32"),
    "ps": ("psum", [P, NL + LC], "float32"),
    "off": ("sbuf", [P, NL], "uint16"),
    "off0": ("sbuf", [P, LC], "uint16"),
    "off1": ("sbuf", [P, LC], "uint16"),
    "tmp": ("sbuf", [P, LC], "float32"),
    "gat": ("sbuf", [P, 4 * CAP], "float32"),
    "gat0": ("sbuf", [P, EB], "float32"),
    "pair": ("sbuf", [P, EB + CAP], "float32"),
    "sel": ("sbuf", [P, LC], "uint16"),
    "land": ("sbuf", [P, 4 * CAP], "float32"),
}
SEMAPHORES = ["l_in", "x0_in", "x1_in", "ones", "rep_ok", "lf_ok", "mm_ok", "prep", "g0_ok", "g_far", "g_near", "g_own",
              "sent", "a_far", "a_n0", "a_n1", "sel_ok", "fin_ok", "st_far", "st_home"]


def _bits(mask):
    return [e for e in range(mask.bit_length()) if (mask >> e) & 1]


def _mask(engines):
    return sum(1 << e for e in engines)


def _runs(ranks):
    out = []
    for r in sorted(ranks):
        if out and out[-1][1] == r:
            out[-1] = (out[-1][0], r + 1)
        else:
            out.append((r, r + 1))
    return out


def _plan(rank, cores, topo):
    me = cores[rank]
    home = lambda c: (topo.host(c), topo.chip(c)) == (topo.host(me), topo.chip(me))
    far = [d for d in range(len(cores)) if d != rank and not home(cores[d])]
    near = [d for d in range(len(cores)) if d != rank and home(cores[d])][0]
    out_eng = _bits(min(topo.mask(me, cores[d]) for d in far))
    k = len(out_eng) // len(far)
    far_plan = [(d, _mask(out_eng[i * k:(i + 1) * k])) for i, d in enumerate(far)]
    every = topo.mask(me, cores[near])
    return far_plan, (near, every, _mask([e for e in _bits(every) if e not in out_eng]))


def rank_program(g, core, T, topo):
    rank = T.rank_of(core)
    if rank is None:
        return
    S, v, cores = T.sem, g.vector, T.cores
    far, (near, m_early, m_late) = _plan(rank, cores, topo)
    blk = lambda t, lo, hi: t[:, CAP * lo:CAP * hi]
    pick = lambda lo, hi: T.xs[:, 0:COLS].indirect(T.off[:, LC * lo:LC * hi])
    nl = T.ps[:, LC * near:LC * (near + 1)]

    g.scalar.dma_start(T.xs[:, 0:C0], T.x[:, 0:C0]).then_inc(S.x0_in, 16)
    g.sync.dma_start(T.li[0:LP, :], T.l[:, :]).then_inc(S.l_in, 16)
    g.scalar.dma_start(T.xs[0:P // 2, C0:COLS], T.x[0:P // 2, C0:COLS]).then_inc(S.x1_in, 16)
    g.sync.dma_start(T.xs[P // 2:P, C0:COLS], T.x[P // 2:P, C0:COLS]).then_inc(S.x1_in, 16)

    v.memset(T.rep[0:LP, :], 1.0).then_inc(S.ones, 1)
    g.iota(T.lf[0:LP, NL:NL + LC], [[LP, LC]], 0, 1, allow_small_or_imprecise_dtypes=True).then_inc(S.rep_ok, 1)
    g.wait_ge(S.ones, 1)
    g.affine_select(T.rep[0:LP, :], T.rep[0:LP, :], [[0, P // LP], [-1, LP]], AluOpType.is_equal, 0.0, 0, 1).then_inc(S.rep_ok, 1)
    v.wait_ge(S.l_in, 16)
    v.tensor_copy(T.lf[0:LP, 0:NL], T.li[0:LP, :]).then_inc(S.lf_ok, 1)
    g.tensor.wait_ge(S.rep_ok, 2)
    g.tensor.wait_ge(S.lf_ok, 1)
    g.tensor.matmul(T.ps[:, :], T.rep[0:LP, :], T.lf[0:LP, :], True, True).then_inc(S.mm_ok, 1)
    v.wait_ge(S.mm_ok, 1)
    v.tensor_scalar(T.off0[:, :], nl, float(C0 - 1), None, AluOpType.min).then_inc(S.prep, 1)
    v.tensor_scalar(T.tmp[:, :], nl, float(C0), float(EB), AluOpType.is_ge, AluOpType.mult).then_inc(S.prep, 1)
    v.tensor_copy(T.off[:, :], T.ps[:, 0:NL]).then_inc(S.prep, 1)
    v.tensor_scalar(T.off1[:, :], nl, float(C0), 0.0, AluOpType.subtract, AluOpType.max).then_inc(S.prep, 1)
    v.wait_ge(S.prep, 4)
    v.tensor_tensor(T.gat0[:, CAP:EB], T.tmp[:, :], T.ps[:, NL:NL + LC], AluOpType.add).then_inc(S.g0_ok, 1)

    v.wait_ge(S.x0_in, 16)
    v.tensor_copy(T.gat0[:, 0:CAP], T.xs[:, 0:C0].indirect(T.off0[:, :])).then_inc(S.g0_ok, 1)
    rid, pid = topo.addr(cores[near], core)
    g.wait_ge(S.g0_ok, 2)
    g.remote_dma(T.pair[:, 0:EB], T.gat0[:, :], S.a_n0, S.sent, pid, rid, m_early)

    v.wait_ge(S.x1_in, 32)
    far_runs = _runs([d for d, _ in far])
    for lo, hi in far_runs:
        v.tensor_copy(blk(T.gat, lo, hi), pick(lo, hi)).then_inc(S.g_far, 1)

    def transfer(d, m):
        r, p = topo.addr(cores[d], core)
        return RemoteDMATransfer(dst_ids=[DstId(rid=r, pnc=p)], dma_engine_mask=m, remote_sem=S.a_far,
                                 src=blk(T.gat, d, d + 1), dst=blk(T.land, rank, rank + 1))
    g.wait_ge(S.g_far, len(far_runs))
    g.remote_dma_fused([transfer(d, m) for d, m in far], local_sem=S.sent)

    v.tensor_copy(blk(T.gat, near, near + 1), T.xs[:, C0:COLS].indirect(T.off1[:, :])).then_inc(S.g_near, 1)
    g.wait_ge(S.g_near, 1)
    g.remote_dma(T.pair[:, EB:EB + CAP], blk(T.gat, near, near + 1), S.a_n1, S.sent, pid, rid, m_late)
    v.tensor_copy(blk(T.land, rank, rank + 1), pick(rank, rank + 1)).then_inc(S.g_own, 1)

    _, (_, n_early, n_late) = _plan(near, cores, topo)
    v.wait_ge(S.a_n0, len(_bits(n_early)))
    v.tensor_copy(T.sel[:, :], T.pair[:, CAP:EB]).then_inc(S.sel_ok, 1)
    v.wait_ge(S.sel_ok, 1)
    v.wait_ge(S.a_n1, len(_bits(n_late)))
    v.tensor_copy(blk(T.land, near, near + 1), T.pair[:, :].indirect(T.sel[:, :])).then_inc(S.fin_ok, 1)

    far_src = [d for d, _ in far]
    g.sync.wait_ge(S.a_far, sum(len(_bits(m)) for s in far_src for d, m in _plan(s, cores, topo)[0] if d == rank))
    n = 0
    for lo, hi in _runs(far_src):
        g.sync.dma_start(blk(T.y, lo, hi), blk(T.land, lo, hi)).then_inc(S.st_far, 16)
        n += 16
    g.sync.wait_ge(S.st_far, n)

    g.scalar.wait_ge(S.g_own, 1)
    g.scalar.wait_ge(S.fin_ok, 1)
    n = 0
    for lo, hi in _runs([near, rank]):
        g.scalar.dma_start(blk(T.y, lo, hi), blk(T.land, lo, hi)).then_inc(S.st_home, 16)
        n += 16
    g.scalar.wait_ge(S.st_home, n)

    g.wait_ge(S.sent, sum(len(_bits(m)) for _, m in far) + len(_bits(m_early)) + len(_bits(m_late)))
